import numpy as np
import ml_dtypes


def mxq(x, axis, fmt="e4m3"):
    dtype, down = {"e4m3": (ml_dtypes.float8_e4m3fn, 7), "e5m2": (ml_dtypes.float8_e5m2, 14)}[fmt]
    v = np.moveaxis(np.asarray(x, np.float32).astype(ml_dtypes.bfloat16).astype(np.float64), axis, -1)
    blocks = v.reshape(v.shape[:-1] + (-1, 32))
    amax = np.abs(blocks).max(-1, keepdims=True)
    byte = np.maximum(np.where(amax > 0, np.frexp(amax)[1] - 1 + 127, 0) - down, 1)
    scale = np.exp2(byte - 127.0)
    codes = (blocks / scale).astype(np.float32).astype(dtype).astype(np.float64)
    return np.moveaxis((codes * scale).reshape(v.shape), -1, axis)


WIDE = False


def mx_kscale(k):
    if not WIDE:
        return np.ones(k)
    levels = np.array([10, -10, 5, -5, 0])
    if k % 512:
        return np.exp2(np.random.permutation(np.resize(levels, k // 32))).repeat(32)
    a = np.empty((k // 512, 16))
    for p in range(k // 512):
        a[p, :8] = np.random.permutation(np.resize(levels, 8))
        for g in range(8):
            far = levels[np.abs(levels - a[p, g]) >= 10]
            a[p, g + 8] = far[np.random.randint(len(far))]
    return np.exp2(a.ravel()).repeat(32)


def f64(x):
    return np.asarray(x).astype(np.float64)


def striped(idx):
    return np.tile(idx.reshape(-1, 16).T, (8, 1)).astype(np.uint16)


def unstriped(offs):
    return offs[:16].T.reshape(-1).astype(np.int64)


E2M1 = np.array([0.0, 0.5, 1.0, 1.5, 2.0, 3.0, 4.0, 6.0, -0.0, -0.5, -1.0, -1.5, -2.0, -3.0, -4.0, -6.0])


def pack_weight(w, fmt):
    k, n = w.shape
    w = f64(np.asarray(w, np.float32).astype(ml_dtypes.bfloat16)).reshape(k // 32, 32, n)
    amax = np.abs(w).max(1)
    if fmt == "e4m3":
        byte = np.frexp(amax)[1] - 1 + 127 - 7
    else:
        mant, ex = np.frexp(amax / 6.0)
        byte = np.where(mant > 0.5, ex, ex - 1) + 127
    byte = np.clip(np.where(amax > 0, byte, 1), 1, 254)
    scaled = (w * np.exp2(127.0 - byte)[:, None, :]).reshape(k, n).astype(np.float32)
    by_word = np.ascontiguousarray(scaled.reshape(k // 512, 128, 4, n).transpose(0, 1, 3, 2))
    if fmt == "e4m3":
        words = by_word.astype(ml_dtypes.float8_e4m3fn).view(np.uint8)
    else:
        c = by_word.astype(ml_dtypes.float4_e2m1fn).view(np.uint8) & 0xF
        words = (c[..., 0::2] | (c[..., 1::2] << 4)).reshape(k // 512, 128, 2 * n)
    return np.ascontiguousarray(words), np.ascontiguousarray(byte.astype(np.uint8).reshape(k // 512, 16, n))


def unpack_weight(words, scales, fmt):
    g, _, n = scales.shape
    words = np.ascontiguousarray(words).reshape(g, 128, n, -1)
    if fmt == "e4m3":
        vals = words.view(ml_dtypes.float8_e4m3fn).astype(np.float64)
    else:
        nib = np.empty((g, 128, n, 4), np.uint8)
        nib[..., 0::2] = words & 0xF
        nib[..., 1::2] = words >> 4
        vals = E2M1[nib]
    vals = vals * np.repeat(np.exp2(scales.astype(np.float64) - 127.0), 8, axis=1)[..., None]
    return vals.transpose(0, 1, 3, 2).reshape(g * 512, n)


def relu2(v):
    return np.maximum(v, 0.0) ** 2


K, T, E, C, N = 512, 4096, 24, 128, 128


def by_expert(wq, xq):
    return np.concatenate([wq[e].T @ xq[:, e * C:(e + 1) * C] for e in range(E)], axis=1)


def setup_inputs():
    n = np.random.standard_normal
    s = mx_kscale(K)[:, None]
    x = pack_weight(n((K, T)) * s, "e4m3")
    return {
        "x_words": x[0],
        "x_scales": x[1],
        "w": (n((E, K, N)) / np.sqrt(K) / s[None]).astype(np.float32),
        "b": (0.3 * n((N, E))).astype(np.float32),
        "gate": np.tile(np.random.uniform(0.2, 1.0, E * C), (N, 1)).astype(np.float32),
        "offs": striped(np.random.permutation(T)[:E * C]),
    }


def reference(x_words, x_scales, w, b, gate, offs):
    idx = unstriped(offs)
    xq = unpack_weight(x_words, x_scales, "e4m3")[:, idx]
    y = by_expert(mxq(f64(w), 1, "e4m3"), xq)
    y = relu2(y + np.repeat(f64(b), C, axis=1))
    out = np.zeros((N, T))
    out[:, idx] = f64(gate) * y
    return out

@@ -1,0 +1,140 @@
+from contextlib import ExitStack
+
+import concourse.mybir as mybir
+
+K, T, E, C, N = 512, 4096, 24, 128, 128
+SLOTS = E * C
+FLOPS = 2 * K * N * SLOTS
+BYTES = 4 * E * K * N + K * T + K * T // 32 + 4 * N * E + 4 * SLOTS + 2 * 128 * SLOTS // 16 + 4 * N * T
+
+F32 = mybir.dt.float32
+BF16 = mybir.dt.bfloat16
+I32 = mybir.dt.int32
+U32 = mybir.dt.uint32
+U16 = mybir.dt.uint16
+U8 = mybir.dt.uint8
+FP8X4 = mybir.dt.float8_e4m3fn_x4
+ACT = mybir.ActivationFunctionType
+MULT = mybir.AluOpType.mult
+
+P = 128
+PACK = 4
+LIST_ROWS = 16
+GROUP = 4
+GROUPS = E // GROUP
+GSLOTS = GROUP * C
+
+
+def tile_moe_pkd_lin_relu2_kernel(tc, x_words, x_scales, w, b, gate, offs, out):
+    nc = tc.nc
+    with ExitStack() as ctx:
+        keep = ctx.enter_context(tc.tile_pool(name="keep", bufs=1))
+        each = ctx.enter_context(tc.tile_pool(name="each", bufs=GROUPS))
+        psum = ctx.enter_context(tc.psum_pool(name="psum", bufs=GROUPS))
+
+        offsets = keep.tile([P, SLOTS // LIST_ROWS], U16)
+        token_words = keep.tile([P, T], I32)
+        token_scales = keep.tile([P, T], U8)
+        slot_words = keep.tile([P, SLOTS], U32, align_bytes=64)
+        slot_scales = keep.tile([P, SLOTS], U8, align_bytes=64)
+        bias = keep.tile([P, E], F32)
+        result = keep.tile([P, T], F32)
+
+        def list_slice(first, count):
+            return offsets[:, first // LIST_ROWS : (first + count) // LIST_ROWS]
+
+        def load_w(g):
+            raw = each.tile([P, GROUP, PACK * N], F32, name="raw")
+            nc.sync.dma_start(raw[:], w[g * GROUP : (g + 1) * GROUP].rearrange("e (p j) n -> p e (j n)", j=PACK))
+            return raw
+
+        def load_gate(g):
+            gates = each.tile([P, GSLOTS], F32, name="gates")
+            nc.sync.dma_start(gates[:], gate[:, g * GSLOTS : (g + 1) * GSLOTS])
+            return gates
+
+        def interleave(raw):
+            staged = each.tile([P, GROUP, N, PACK], BF16, name="staged", align_bytes=64)
+            nc.scalar.copy(
+                staged[:].rearrange("p e (c i) j -> p e c j i", i=4),
+                raw[:].rearrange("p e (j c i) -> p e c j i", j=PACK, i=4),
+            )
+            return staged
+
+        def multiply(g, staged):
+            codes = each.tile([P, GROUP * N], U32, name="codes", align_bytes=64)
+            scales = each.tile([P, GROUP * N], U8, name="scales", align_bytes=64)
+            nc.vector.quantize_mx(
+                out=codes[:].bitcast(FP8X4), scales=scales[:], in_=staged[:].rearrange("p e n j -> p (e n j)")
+            )
+            return codes, scales
+
+        def matmuls(g, codes, scales):
+            acc = psum.tile([P, GSLOTS], F32, name="acc")
+            for j in range(GROUP):
+                cols = slice(j * N, (j + 1) * N)
+                slots = slice(g * GSLOTS + j * C, g * GSLOTS + (j + 1) * C)
+                nc.tensor.matmul_mx(
+                    out=acc[:, j * C : (j + 1) * C],
+                    lhsT=codes[:, cols].bitcast(FP8X4),
+                    lhsT_scale=scales[:, cols],
+                    rhs=slot_words[:, slots].bitcast(FP8X4),
+                    rhs_scale=slot_scales[:, slots],
+                    start=True,
+                    stop=True,
+                )
+            return acc
+
+        def relu2(g, acc):
+            rect = each.tile([P, GSLOTS], F32, name="rect")
+            for j in range(GROUP):
+                e = g * GROUP + j
+                nc.scalar.activation(
+                    rect[:, j * C : (j + 1) * C], acc[:, j * C : (j + 1) * C], ACT.Relu, bias=bias[:, e : e + 1]
+                )
+            squared = each.tile([P, GSLOTS], F32, name="squared")
+            nc.scalar.activation(squared[:], rect[:], ACT.Square)
+            return squared
+
+        def scatter(g, squared, gates):
+            nc.vector.tensor_tensor(result[:].indirect(list_slice(g * GSLOTS, GSLOTS)), squared[:], gates[:], MULT)
+
+        nc.sync.dma_start(offsets[:], offs)
+        for q in range(4):
+            rows = x_scales[0, 4 * q : 4 * q + 4, :].bitcast(I32)
+            nc.sync.dma_start(token_scales[32 * q : 32 * q + 32, :].bitcast(I32), rows.partition_broadcast(8))
+        zero = keep.tile([P, 1], F32)
+        nc.vector.memset(zero[:], 0.0)
+        nc.scalar.copy(result[:], zero[:].to_broadcast([P, T]))
+        raws = [load_w(0)]
+        nc.sync.dma_start(token_words[:], x_words[0].rearrange("p t r -> p (t r)").bitcast(I32))
+        nc.sync.dma_start(bias[:], b)
+        gates = []
+        for g in range(1, GROUPS):
+            raws.append(load_w(g))
+            if g >= 2:
+                gates.append(load_gate(g - 2))
+        for g in range(GROUPS - 2, GROUPS):
+            gates.append(load_gate(g))
+
+        for first in range(0, SLOTS, SLOTS // 2):
+            nc.vector.tensor_copy(
+                slot_scales[:, first : first + SLOTS // 2], token_scales[:].indirect(list_slice(first, SLOTS // 2))
+            )
+        quantised = multiply(0, interleave(raws[0]))
+        first = 0
+        for count in (GSLOTS, 2 * GSLOTS, 3 * GSLOTS):
+            nc.vector.tensor_copy(
+                slot_words[:, first : first + count], token_words[:].bitcast(U32).indirect(list_slice(first, count))
+            )
+            first = first + count
+        acc = matmuls(0, *quantised)
+        for g in range(GROUPS):
+            if g + 1 < GROUPS:
+                quantised = multiply(g + 1, interleave(raws[g + 1]))
+            squared = relu2(g, acc)
+            if g + 1 < GROUPS:
+                acc = matmuls(g + 1, *quantised)
+            scatter(g, squared, gates[g])
+
+        nc.sync.dma_start(out, result[:])

@@ -49,7 +49,7 @@ def tile_moe_pkd_lin_relu2_kernel(tc, x_words, x_scales, w, b, gate, offs, out):
             return raw
 
         def load_gate(g):
-            gates = each.tile([P, GSLOTS], F32, name="gates")
+            gates = keep.tile([P, GSLOTS], F32, name=f"gates{g}", tag=f"turn{g + 2}", align_bytes=64)
             nc.sync.dma_start(gates[:], gate[:, g * GSLOTS : (g + 1) * GSLOTS])
             return gates
 
@@ -62,7 +62,7 @@ def tile_moe_pkd_lin_relu2_kernel(tc, x_words, x_scales, w, b, gate, offs, out):
             return staged
 
         def multiply(g, staged):
-            codes = each.tile([P, GROUP * N], U32, name="codes", align_bytes=64)
+            codes = keep.tile([P, GROUP * N], U32, name=f"codes{g}", tag=f"turn{g}", align_bytes=64)
             scales = each.tile([P, GROUP * N], U8, name="scales", align_bytes=64)
             nc.vector.quantize_mx(
                 out=codes[:].bitcast(FP8X4), scales=scales[:], in_=staged[:].rearrange("p e n j -> p (e n j)")

@@ -49,7 +49,7 @@ def tile_moe_pkd_lin_relu2_kernel(tc, x_words, x_scales, w, b, gate, offs, out):
             return raw
 
         def load_gate(g):
-            gates = keep.tile([P, GSLOTS], F32, name=f"gates{g}", tag=f"turn{g + 2}", align_bytes=64)
+            gates = each.tile([P, GSLOTS], F32, name="gates")
             nc.sync.dma_start(gates[:], gate[:, g * GSLOTS : (g + 1) * GSLOTS])
             return gates
 
@@ -62,7 +62,7 @@ def tile_moe_pkd_lin_relu2_kernel(tc, x_words, x_scales, w, b, gate, offs, out):
             return staged
 
         def multiply(g, staged):
-            codes = keep.tile([P, GROUP * N], U32, name=f"codes{g}", tag=f"turn{g}", align_bytes=64)
+            codes = each.tile([P, GROUP * N], U32, name="codes", align_bytes=64)
             scales = each.tile([P, GROUP * N], U8, name="scales", align_bytes=64)
             nc.vector.quantize_mx(
                 out=codes[:].bitcast(FP8X4), scales=scales[:], in_=staged[:].rearrange("p e n j -> p (e n j)")
@@ -99,16 +99,20 @@ def tile_moe_pkd_lin_relu2_kernel(tc, x_words, x_scales, w, b, gate, offs, out):
         def scatter(g, squared, gates):
             nc.vector.tensor_tensor(result[:].indirect(list_slice(g * GSLOTS, GSLOTS)), squared[:], gates[:], MULT)
 
+        nc.vector.memset(token_scales[:, 0 : T // 2].bitcast(I32), 0)
+        nc.gpsimd.memset(token_scales[:, T // 2 : T].bitcast(I32), 0)
         nc.sync.dma_start(offsets[:], offs)
-        for q in range(4):
-            rows = x_scales[0, 4 * q : 4 * q + 4, :].bitcast(I32)
-            nc.sync.dma_start(token_scales[32 * q : 32 * q + 32, :].bitcast(I32), rows.partition_broadcast(8))
+        for r in range(PACK):
+            nc.sync.dma_start(token_scales[r:P:32, :].bitcast(I32), x_scales[0, r:16:4, :].bitcast(I32))
+        nc.sync.dma_start(bias[:], b)
         zero = keep.tile([P, 1], F32)
         nc.vector.memset(zero[:], 0.0)
         nc.scalar.copy(result[:], zero[:].to_broadcast([P, T]))
-        raws = [load_w(0)]
+        raw0 = each.tile([P, GROUP, PACK * N], F32, name="raw")
+        for e in range(GROUP):
+            nc.sync.dma_start(raw0[:, e, :], w[e].rearrange("(p j) n -> p (j n)", j=PACK))
+        raws = [raw0]
         nc.sync.dma_start(token_words[:], x_words[0].rearrange("p t r -> p (t r)").bitcast(I32))
-        nc.sync.dma_start(bias[:], b)
         gates = []
         for g in range(1, GROUPS):
             raws.append(load_w(g))

@@ -39,6 +39,8 @@ def tile_moe_pkd_lin_relu2_kernel(tc, x_words, x_scales, w, b, gate, offs, out):
         slot_scales = keep.tile([P, SLOTS], U8, align_bytes=64)
         bias = keep.tile([P, E], F32)
         result = keep.tile([P, T], F32)
+        gates = keep.tile([P, SLOTS], F32)
+        squared = keep.tile([P, SLOTS], F32)
 
         def list_slice(first, count):
             return offsets[:, first // LIST_ROWS : (first + count) // LIST_ROWS]
@@ -49,9 +51,7 @@ def tile_moe_pkd_lin_relu2_kernel(tc, x_words, x_scales, w, b, gate, offs, out):
             return raw
 
         def load_gate(g):
-            gates = each.tile([P, GSLOTS], F32, name="gates")
-            nc.sync.dma_start(gates[:], gate[:, g * GSLOTS : (g + 1) * GSLOTS])
-            return gates
+            nc.sync.dma_start(gates[:, g * GSLOTS : (g + 1) * GSLOTS], gate[:, g * GSLOTS : (g + 1) * GSLOTS])
 
         def interleave(raw):
             staged = each.tile([P, GROUP, N, PACK], BF16, name="staged", align_bytes=64)
@@ -92,12 +92,13 @@ def tile_moe_pkd_lin_relu2_kernel(tc, x_words, x_scales, w, b, gate, offs, out):
                 nc.scalar.activation(
                     rect[:, j * C : (j + 1) * C], acc[:, j * C : (j + 1) * C], ACT.Relu, bias=bias[:, e : e + 1]
                 )
-            squared = each.tile([P, GSLOTS], F32, name="squared")
-            nc.scalar.activation(squared[:], rect[:], ACT.Square)
-            return squared
+            nc.scalar.activation(squared[:, g * GSLOTS : (g + 1) * GSLOTS], rect[:], ACT.Square)
 
-        def scatter(g, squared, gates):
-            nc.vector.tensor_tensor(result[:].indirect(list_slice(g * GSLOTS, GSLOTS)), squared[:], gates[:], MULT)
+        def scatter(first, count):
+            slots = slice(first, first + count)
+            nc.vector.tensor_tensor(
+                result[:].indirect(list_slice(first, count)), squared[:, slots], gates[:, slots], MULT
+            )
 
         nc.vector.memset(token_scales[:, 0 : T // 2].bitcast(I32), 0)
         nc.gpsimd.memset(token_scales[:, T // 2 : T].bitcast(I32), 0)
@@ -109,17 +110,18 @@ def tile_moe_pkd_lin_relu2_kernel(tc, x_words, x_scales, w, b, gate, offs, out):
         nc.vector.memset(zero[:], 0.0)
         nc.scalar.copy(result[:], zero[:].to_broadcast([P, T]))
         raw0 = each.tile([P, GROUP, PACK * N], F32, name="raw")
-        for e in range(GROUP):
-            nc.sync.dma_start(raw0[:, e, :], w[e].rearrange("(p j) n -> p (j n)", j=PACK))
+        first_expert = w[0].rearrange("(p j) n -> p (j n)", j=PACK)
+        for half in (slice(0, 2 * N), slice(2 * N, 4 * N)):
+            nc.sync.dma_start(raw0[:, 0, half], first_expert[:, half])
+        nc.sync.dma_start(raw0[:, 1:GROUP, :], w[1:GROUP].rearrange("e (p j) n -> p e (j n)", j=PACK))
         raws = [raw0]
         nc.sync.dma_start(token_words[:], x_words[0].rearrange("p t r -> p (t r)").bitcast(I32))
-        gates = []
         for g in range(1, GROUPS):
             raws.append(load_w(g))
             if g >= 2:
-                gates.append(load_gate(g - 2))
+                load_gate(g - 2)
         for g in range(GROUPS - 2, GROUPS):
-            gates.append(load_gate(g))
+            load_gate(g)
 
         for first in range(0, SLOTS, SLOTS // 2):
             nc.vector.tensor_copy(
@@ -136,9 +138,12 @@ def tile_moe_pkd_lin_relu2_kernel(tc, x_words, x_scales, w, b, gate, offs, out):
         for g in range(GROUPS):
             if g + 1 < GROUPS:
                 quantised = multiply(g + 1, interleave(raws[g + 1]))
-            squared = relu2(g, acc)
+            relu2(g, acc)
             if g + 1 < GROUPS:
                 acc = matmuls(g + 1, *quantised)
-            scatter(g, squared, gates[g])
+            if g < GROUPS - 2:
+                scatter(g * GSLOTS, GSLOTS)
+        scatter((GROUPS - 2) * GSLOTS, 2 * GSLOTS)
 
-        nc.sync.dma_start(out, result[:])
+        nc.sync.dma_start(out[:, 0 : T // 2], result[:, 0 : T // 2])
+        nc.scalar.dma_start(out[:, T // 2 : T], result[:, T // 2 : T])

from contextlib import ExitStack

import concourse.mybir as mybir

K, T, E, C, N = 512, 4096, 24, 128, 128
SLOTS = E * C
FLOPS = 2 * K * N * SLOTS
BYTES = 4 * E * K * N + K * T + K * T // 32 + 4 * N * E + 4 * SLOTS + 2 * 128 * SLOTS // 16 + 4 * N * T

F32 = mybir.dt.float32
BF16 = mybir.dt.bfloat16
I32 = mybir.dt.int32
U32 = mybir.dt.uint32
U16 = mybir.dt.uint16
U8 = mybir.dt.uint8
FP8X4 = mybir.dt.float8_e4m3fn_x4
ACT = mybir.ActivationFunctionType
MULT = mybir.AluOpType.mult

P = 128
PACK = 4
LIST_ROWS = 16
GROUP = 4
GROUPS = E // GROUP
GSLOTS = GROUP * C


def tile_moe_pkd_lin_relu2_kernel(tc, x_words, x_scales, w, b, gate, offs, out):
    nc = tc.nc
    with ExitStack() as ctx:
        keep = ctx.enter_context(tc.tile_pool(name="keep", bufs=1))
        each = ctx.enter_context(tc.tile_pool(name="each", bufs=GROUPS))
        psum = ctx.enter_context(tc.psum_pool(name="psum", bufs=GROUPS))

        offsets = keep.tile([P, SLOTS // LIST_ROWS], U16)
        token_words = keep.tile([P, T], I32)
        token_scales = keep.tile([P, T], U8)
        slot_words = keep.tile([P, SLOTS], U32, align_bytes=64)
        slot_scales = keep.tile([P, SLOTS], U8, align_bytes=64)
        bias = keep.tile([P, E], F32)
        result = keep.tile([P, T], F32)
        gates = keep.tile([P, SLOTS], F32)
        squared = keep.tile([P, SLOTS], F32)

        def list_slice(first, count):
            return offsets[:, first // LIST_ROWS : (first + count) // LIST_ROWS]

        def load_w(g):
            raw = each.tile([P, GROUP, PACK * N], F32, name="raw")
            nc.sync.dma_start(raw[:], w[g * GROUP : (g + 1) * GROUP].rearrange("e (p j) n -> p e (j n)", j=PACK))
            return raw

        def load_gate(g):
            nc.sync.dma_start(gates[:, g * GSLOTS : (g + 1) * GSLOTS], gate[:, g * GSLOTS : (g + 1) * GSLOTS])

        def interleave(raw):
            staged = each.tile([P, GROUP, N, PACK], BF16, name="staged", align_bytes=64)
            nc.scalar.copy(
                staged[:].rearrange("p e (c i) j -> p e c j i", i=4),
                raw[:].rearrange("p e (j c i) -> p e c j i", j=PACK, i=4),
            )
            return staged

        def multiply(g, staged):
            codes = each.tile([P, GROUP * N], U32, name="codes", align_bytes=64)
            scales = each.tile([P, GROUP * N], U8, name="scales", align_bytes=64)
            nc.vector.quantize_mx(
                out=codes[:].bitcast(FP8X4), scales=scales[:], in_=staged[:].rearrange("p e n j -> p (e n j)")
            )
            return codes, scales

        def matmuls(g, codes, scales):
            acc = psum.tile([P, GSLOTS], F32, name="acc")
            for j in range(GROUP):
                cols = slice(j * N, (j + 1) * N)
                slots = slice(g * GSLOTS + j * C, g * GSLOTS + (j + 1) * C)
                nc.tensor.matmul_mx(
                    out=acc[:, j * C : (j + 1) * C],
                    lhsT=codes[:, cols].bitcast(FP8X4),
                    lhsT_scale=scales[:, cols],
                    rhs=slot_words[:, slots].bitcast(FP8X4),
                    rhs_scale=slot_scales[:, slots],
                    start=True,
                    stop=True,
                )
            return acc

        def relu2(g, acc):
            rect = each.tile([P, GSLOTS], F32, name="rect")
            for j in range(GROUP):
                e = g * GROUP + j
                nc.scalar.activation(
                    rect[:, j * C : (j + 1) * C], acc[:, j * C : (j + 1) * C], ACT.Relu, bias=bias[:, e : e + 1]
                )
            nc.scalar.activation(squared[:, g * GSLOTS : (g + 1) * GSLOTS], rect[:], ACT.Square)

        def scatter(first, count):
            slots = slice(first, first + count)
            nc.vector.tensor_tensor(
                result[:].indirect(list_slice(first, count)), squared[:, slots], gates[:, slots], MULT
            )

        nc.vector.memset(token_scales[:, 0 : T // 2].bitcast(I32), 0)
        nc.gpsimd.memset(token_scales[:, T // 2 : T].bitcast(I32), 0)
        nc.sync.dma_start(offsets[:], offs)
        for r in range(PACK):
            nc.sync.dma_start(token_scales[r:P:32, :].bitcast(I32), x_scales[0, r:16:4, :].bitcast(I32))
        nc.sync.dma_start(bias[:], b)
        zero = keep.tile([P, 1], F32)
        nc.vector.memset(zero[:], 0.0)
        nc.scalar.copy(result[:], zero[:].to_broadcast([P, T]))
        raw0 = each.tile([P, GROUP, PACK * N], F32, name="raw")
        first_expert = w[0].rearrange("(p j) n -> p (j n)", j=PACK)
        for half in (slice(0, 2 * N), slice(2 * N, 4 * N)):
            nc.sync.dma_start(raw0[:, 0, half], first_expert[:, half])
        nc.sync.dma_start(raw0[:, 1:GROUP, :], w[1:GROUP].rearrange("e (p j) n -> p e (j n)", j=PACK))
        raws = [raw0]
        nc.sync.dma_start(token_words[:], x_words[0].rearrange("p t r -> p (t r)").bitcast(I32))
        for g in range(1, GROUPS):
            raws.append(load_w(g))
            if g >= 2:
                load_gate(g - 2)
        for g in range(GROUPS - 2, GROUPS):
            load_gate(g)

        for first in range(0, SLOTS, SLOTS // 2):
            nc.vector.tensor_copy(
                slot_scales[:, first : first + SLOTS // 2], token_scales[:].indirect(list_slice(first, SLOTS // 2))
            )
        quantised = multiply(0, interleave(raws[0]))
        first = 0
        for count in (GSLOTS, 2 * GSLOTS, 3 * GSLOTS):
            nc.vector.tensor_copy(
                slot_words[:, first : first + count], token_words[:].bitcast(U32).indirect(list_slice(first, count))
            )
            first = first + count
        acc = matmuls(0, *quantised)
        for g in range(GROUPS):
            if g + 1 < GROUPS:
                quantised = multiply(g + 1, interleave(raws[g + 1]))
            relu2(g, acc)
            if g + 1 < GROUPS:
                acc = matmuls(g + 1, *quantised)
            if g < GROUPS - 2:
                scatter(g * GSLOTS, GSLOTS)
        scatter((GROUPS - 2) * GSLOTS, 2 * GSLOTS)

        nc.sync.dma_start(out[:, 0 : T // 2], result[:, 0 : T // 2])
        nc.scalar.dma_start(out[:, T // 2 : T], result[:, T // 2 : T])
